import numpy as np
import ml_dtypes


def mxq(x, axis, fmt="e4m3"):
    dtype, down = {"e4m3": (ml_dtypes.float8_e4m3fn, 7), "e5m2": (ml_dtypes.float8_e5m2, 14)}[fmt]
    v = np.moveaxis(np.asarray(x, np.float32).astype(ml_dtypes.bfloat16).astype(np.float64), axis, -1)
    blocks = v.reshape(v.shape[:-1] + (-1, 32))
    amax = np.abs(blocks).max(-1, keepdims=True)
    byte = np.maximum(np.where(amax > 0, np.frexp(amax)[1] - 1 + 127, 0) - down, 1)
    scale = np.exp2(byte - 127.0)
    codes = (blocks / scale).astype(np.float32).astype(dtype).astype(np.float64)
    return np.moveaxis((codes * scale).reshape(v.shape), -1, axis)


WIDE = False


def mx_kscale(k):
    if not WIDE:
        return np.ones(k)
    levels = np.array([10, -10, 5, -5, 0])
    if k % 512:
        return np.exp2(np.random.permutation(np.resize(levels, k // 32))).repeat(32)
    a = np.empty((k // 512, 16))
    for p in range(k // 512):
        a[p, :8] = np.random.permutation(np.resize(levels, 8))
        for g in range(8):
            far = levels[np.abs(levels - a[p, g]) >= 10]
            a[p, g + 8] = far[np.random.randint(len(far))]
    return np.exp2(a.ravel()).repeat(32)


def f64(x):
    return np.asarray(x).astype(np.float64)


def striped(idx):
    return np.tile(idx.reshape(-1, 16).T, (8, 1)).astype(np.uint16)


def unstriped(offs):
    return offs[:16].T.reshape(-1).astype(np.int64)


E2M1 = np.array([0.0, 0.5, 1.0, 1.5, 2.0, 3.0, 4.0, 6.0, -0.0, -0.5, -1.0, -1.5, -2.0, -3.0, -4.0, -6.0])


def pack_weight(w, fmt):
    k, n = w.shape
    w = f64(np.asarray(w, np.float32).astype(ml_dtypes.bfloat16)).reshape(k // 32, 32, n)
    amax = np.abs(w).max(1)
    if fmt == "e4m3":
        byte = np.frexp(amax)[1] - 1 + 127 - 7
    else:
        mant, ex = np.frexp(amax / 6.0)
        byte = np.where(mant > 0.5, ex, ex - 1) + 127
    byte = np.clip(np.where(amax > 0, byte, 1), 1, 254)
    scaled = (w * np.exp2(127.0 - byte)[:, None, :]).reshape(k, n).astype(np.float32)
    by_word = np.ascontiguousarray(scaled.reshape(k // 512, 128, 4, n).transpose(0, 1, 3, 2))
    if fmt == "e4m3":
        words = by_word.astype(ml_dtypes.float8_e4m3fn).view(np.uint8)
    else:
        c = by_word.astype(ml_dtypes.float4_e2m1fn).view(np.uint8) & 0xF
        words = (c[..., 0::2] | (c[..., 1::2] << 4)).reshape(k // 512, 128, 2 * n)
    return np.ascontiguousarray(words), np.ascontiguousarray(byte.astype(np.uint8).reshape(k // 512, 16, n))


def unpack_weight(words, scales, fmt):
    g, _, n = scales.shape
    words = np.ascontiguousarray(words).reshape(g, 128, n, -1)
    if fmt == "e4m3":
        vals = words.view(ml_dtypes.float8_e4m3fn).astype(np.float64)
    else:
        nib = np.empty((g, 128, n, 4), np.uint8)
        nib[..., 0::2] = words & 0xF
        nib[..., 1::2] = words >> 4
        vals = E2M1[nib]
    vals = vals * np.repeat(np.exp2(scales.astype(np.float64) - 127.0), 8, axis=1)[..., None]
    return vals.transpose(0, 1, 3, 2).reshape(g * 512, n)


def gelu(v):
    return 0.5 * v * (1.0 + np.tanh(np.sqrt(2.0 / np.pi) * (v + 0.044715 * v**3)))


K, R, H, T, S, T2, S2, T3, P = 1024, 512, 512, 4096, 1024, 2048, 1024, 2048, 512

def setup_inputs():
    n = np.random.standard_normal
    s = mx_kscale(K)[:, None]
    d = mx_kscale(R)[:, None]
    u = mx_kscale(H)[:, None]
    tab_words, tab_scales = pack_weight(n((K, T)) * s, "e4m3")
    tab2_words, tab2_scales = pack_weight(n((H, T3)) / np.sqrt(H) / u, "e4m3")
    w3_words, w3_scales = pack_weight(0.7 * n((K, H)) / np.sqrt(K) / s * u.T, "e2m1")
    qry_words, qry_scales = pack_weight(n((H, P)) * u, "e4m3")
    return {
        "tab_words": tab_words, "tab_scales": tab_scales,
        "tab2_words": tab2_words, "tab2_scales": tab2_scales,
        "w1": (1.8 * n((K, R)) / np.sqrt(K) / s).astype(np.float32),
        "tgain": (np.exp(0.3 * n(R)) * d[:, 0]).astype(np.float32),
        "w2": (1.3 * n((R, H)) / np.sqrt(R) / d * u.T).astype(np.float32),
        "w3_words": w3_words, "w3_scales": w3_scales,
        "gain": np.exp(0.3 * n(H)).astype(np.float32),
        "page0": (n((H, T2)) * u).astype(np.float32),
        "wgs": np.exp(0.3 * n((128, S))).astype(np.float32),
        "mat": (1.0 + 0.5 * n((H, P))).astype(np.float32),
        "qry_words": qry_words, "qry_scales": qry_scales,
        "cand": (0.5 * n(S2)).astype(np.float32),
        "offs": striped(np.random.permutation(T)[:S]), "offs2": striped(np.random.permutation(T3)[:S2]),
        "offs3": striped(np.random.permutation(T2)[:S]), "offs4": striped(np.random.permutation(T2)[:P])}

def reference(tab_words, tab_scales, tab2_words, tab2_scales, w1, tgain, w2, w3_words, w3_scales, gain, page0, wgs, mat, qry_words, qry_scales, cand, offs, offs2, offs3, offs4):
    v = unpack_weight(tab_words, tab_scales, "e4m3")[:, unstriped(offs)]
    v2 = unpack_weight(tab2_words, tab2_scales, "e4m3")[:, unstriped(offs2)]
    w3 = unpack_weight(w3_words, w3_scales, "e2m1")
    qry = unpack_weight(qry_words, qry_scales, "e4m3")
    act = np.tanh(mxq(f64(w1), 0, "e4m3").T @ v) * f64(tgain)[:, None]
    h = (mxq(f64(w2), 0, "e4m3").T @ mxq(act, 0, "e4m3") + w3.T @ v) * f64(gain)[:, None]
    page = f64(page0).copy()
    page[:, unstriped(offs3)] = np.tile(f64(wgs), (H // 128, 1)) * h
    x = page[:, unstriped(offs4)] * f64(mat)
    e = v2.T @ mxq(x, 0, "e4m3")
    f = v2.T @ qry
    return np.maximum(e, f) + f64(cand)[:, None]

@@ -1,0 +1,336 @@
+from contextlib import ExitStack
+
+import concourse.mybir as mybir
+from concourse.masks import make_identity
+
+K, R, H, T, S, T2, S2, T3, NJ = 1024, 512, 512, 4096, 1024, 2048, 1024, 2048, 512
+FLOPS = 2 * (K * R * S + R * H * S + K * H * S + 2 * H * S2 * NJ)
+
+F32 = mybir.dt.float32
+BF16 = mybir.dt.bfloat16
+I32 = mybir.dt.int32
+U32 = mybir.dt.uint32
+U16 = mybir.dt.uint16
+U8 = mybir.dt.uint8
+FP8X4 = mybir.dt.float8_e4m3fn_x4
+FP4X4 = mybir.dt.float4_e2m1fn_x4
+ACT = mybir.ActivationFunctionType
+ALU = mybir.AluOpType
+
+P = 128
+PACK = 4
+PASS = P * PACK
+QUAD = 32
+QN = 256
+NQ = S // QN
+CH = 128
+
+
+def tile_list_mailbox_suggestion_scores_kernel(
+    tc, tab_words, tab_scales, tab2_words, tab2_scales, w1, tgain, w2, w3_words, w3_scales, gain,
+    page0, wgs, mat, qry_words, qry_scales, cand, offs, offs2, offs3, offs4, out,
+):
+    nc = tc.nc
+    with ExitStack() as ctx:
+        lists = ctx.enter_context(tc.tile_pool(name="lists", bufs=1))
+        keep = ctx.enter_context(tc.tile_pool(name="keep", bufs=1))
+        ring = ctx.enter_context(tc.tile_pool(name="ring", bufs=2))
+        psum = ctx.enter_context(tc.psum_pool(name="psum", bufs=1))
+
+        def held(name, shape, dtype, tag=None):
+            return keep.tile(shape, dtype, name=name, tag=tag or name, align_bytes=64)
+
+        def ringed(name, shape, dtype, bufs=2):
+            return ring.tile(shape, dtype, name=name, tag=name, bufs=bufs, align_bytes=64)
+
+        def bank(tag, shape, bufs):
+            return psum.tile(shape, F32, name=tag, tag=tag, bufs=bufs)
+
+        def words_of(dram):
+            return dram.rearrange("p n i -> p (n i)").bitcast(I32)
+
+        idx = lists.tile([P, S // 16], U16, name="idx")
+        idx2 = lists.tile([P, S2 // 16], U16, name="idx2")
+        idx3 = lists.tile([P, S // 16], U16, name="idx3")
+        idx4 = lists.tile([P, NJ // 16], U16, name="idx4")
+
+        tab_w = [held("tab_w%d" % a, [P, T], U32) for a in range(2)]
+        tab_s = held("tab_s", [P, T], U8)
+        tab2_w = held("tab2_w", [P, T3], U32)
+        tab2_s = held("tab2_s", [P, T3], U8)
+        w3_raw = held("w3_raw", [P, 2, 2 * H], U8)
+        w3s_raw = held("w3s_raw", [P, 2, H], U8)
+        v_s1 = held("v_s1", [P, S], U8)
+        qry_w = held("qry_w", [P, NJ], U32)
+        qry_s = held("qry_s", [P, NJ], U8)
+        cand_rows = held("cand_rows", [P, P], F32)
+        ident = held("ident", [P, P], F32)
+        wgs_raw = held("wgs_raw", [P, S], F32)
+        tg = held("tg", [P, PACK], F32)
+        gn = held("gn", [P, PACK], F32)
+        w1_raw = [held("w1_raw%d" % a, [P, PACK, R], F32) for a in range(2)]
+        w2_raw = held("w2_raw", [P, PACK, H], F32)
+        page = [held("page%d" % t, [P, T2], F32) for t in range(PACK)]
+        mat_sb = held("mat_sb", [P, PACK, NJ], F32)
+
+        for plane in (tab2_s, tab_s, w3s_raw, v_s1, qry_s):
+            nc.vector.memset(plane[:].bitcast(I32), 0)
+        nc.vector.memset(cand_rows[:], 0.0)
+        make_identity(nc, ident[:])
+
+        for quad in range(4):
+            nc.gpsimd.dma_start(
+                out=tab2_s[QUAD * quad : QUAD * quad + 4, :].bitcast(I32),
+                in_=tab2_scales[0, 4 * quad : 4 * quad + 4, :].bitcast(I32),
+            )
+        for quad in range(4):
+            nc.gpsimd.dma_start(
+                out=tab_s[QUAD * quad : QUAD * quad + 8, :].bitcast(I32),
+                in_=tab_scales[:, 4 * quad : 4 * quad + 4, :].bitcast(I32),
+            )
+
+        nc.sync.dma_start(idx2[:], offs2)
+        nc.sync.dma_start(out=tab2_w[:].bitcast(I32), in_=words_of(tab2_words[0]))
+        nc.sync.dma_start(out=wgs_raw[:], in_=wgs)
+        nc.sync.dma_start(out=gn[:], in_=gain.rearrange("(p t) -> p t", t=PACK))
+        nc.sync.dma_start(out=w3_raw[:].bitcast(I32), in_=w3_words.rearrange("a p b -> p a b").bitcast(I32))
+        nc.sync.dma_start(idx[:], offs)
+        for a in range(2):
+            nc.sync.dma_start(out=tab_w[a][:].bitcast(I32), in_=words_of(tab_words[a]))
+        for quad in range(4):
+            nc.sync.dma_start(
+                out=w3s_raw[QUAD * quad : QUAD * quad + 4, :, :].bitcast(I32),
+                in_=w3_scales[:, 4 * quad : 4 * quad + 4, :].rearrange("a r c -> r a c").bitcast(I32),
+            )
+        nc.sync.dma_start(out=tg[:], in_=tgain.rearrange("(p t) -> p t", t=PACK))
+        for a in range(2):
+            nc.sync.dma_start(
+                out=w1_raw[a][:], in_=w1[a * PASS : (a + 1) * PASS, :].rearrange("(p j) c -> p j c", j=PACK)
+            )
+        nc.sync.dma_start(idx3[:], offs3)
+        nc.sync.dma_start(out=w2_raw[:], in_=w2.rearrange("(p j) c -> p j c", j=PACK))
+        page_rows = page0.rearrange("(p t) s -> p t s", t=PACK)
+        for t in range(PACK):
+            nc.sync.dma_start(out=page[t][:], in_=page_rows[:, t, :])
+        nc.sync.dma_start(out=qry_w[:].bitcast(I32), in_=words_of(qry_words[0]))
+        for quad in range(4):
+            nc.sync.dma_start(
+                out=qry_s[QUAD * quad : QUAD * quad + 4, :].bitcast(I32),
+                in_=qry_scales[0, 4 * quad : 4 * quad + 4, :].bitcast(I32),
+            )
+        nc.sync.dma_start(out=cand_rows[0 : S2 // P, :], in_=cand.rearrange("(i p) -> i p", p=P))
+        nc.sync.dma_start(idx4[:], offs4)
+        nc.sync.dma_start(out=mat_sb[:], in_=mat.rearrange("(p t) j -> p t j", t=PACK))
+
+        v2_w = held("v2_w", [P, S2], U32)
+        v2_s = held("v2_s", [P, S2], U8)
+        v_w = [held("v_w%d" % a, [P, S], U32) for a in range(2)]
+        v_s = held("v_s", [P, S], U8)
+        w3_d = held("w3_d", [P, 2, 2 * H], U8)
+        w3s_d = held("w3s_d", [P, 2, H], U8)
+        nc.vector.tensor_copy(v2_w[:], tab2_w[:].indirect(idx2[:]))
+        nc.vector.tensor_copy(v_s[:], tab_s[:].indirect(idx[:]))
+        for quad in range(4):
+            nc.gpsimd.dma_start(
+                out=v_s1[QUAD * quad : QUAD * quad + 4, :].bitcast(I32),
+                in_=v_s[QUAD * quad + 4 : QUAD * quad + 8, :].bitcast(I32),
+            )
+        for a in range(2):
+            nc.vector.tensor_copy(v_w[a][:], tab_w[a][:].indirect(idx[:]))
+        nc.vector.tensor_copy(v2_s[:], tab2_s[:].indirect(idx2[:]))
+        nc.vector.tensor_copy(
+            out=w3_d[:].bitcast(U16).rearrange("p a (t m) -> p a t m", t=PACK),
+            in_=w3_raw[:].bitcast(U16).rearrange("p a (m t) -> p a t m", t=PACK),
+        )
+        nc.vector.tensor_copy(
+            out=w3s_d[:].rearrange("p a (t m) -> p a t m", t=PACK),
+            in_=w3s_raw[:].rearrange("p a (m t) -> p a t m", t=PACK),
+        )
+
+        wg = held("wg", [P, PACK, S], F32)
+        for half in range(2):
+            turned = bank("misc", [P, 4, CH], 4)
+            for c in range(4):
+                col = (4 * half + c) * CH
+                nc.tensor.transpose(turned[:, c, :], wgs_raw[:, col : col + CH], ident[:])
+            spread = []
+            for c in range(4):
+                rep = ringed("rep", [P, PACK, 4, QUAD], F32, bufs=4)
+                nc.scalar.copy(
+                    out=rep[:],
+                    in_=turned[:, c, :].rearrange("j (m t) -> j t m", t=PACK).unsqueeze(2).to_broadcast([P, PACK, 4, QUAD]),
+                )
+                spread.append(rep)
+            for t in range(PACK):
+                back = bank("misc", [P, 4, CH], 4)
+                for c in range(4):
+                    nc.tensor.transpose(back[:, c, :], spread[c][:, t, :, :].rearrange("j q m -> j (q m)"), ident[:])
+                nc.scalar.activation(
+                    out=wg[:, t, half * 512 : (half + 1) * 512], in_=back[:].rearrange("p c j -> p (c j)"),
+                    func=ACT.Copy, scale=gn[:, t : t + 1],
+                )
+
+        def deal(engine_copy, raw, name, tag):
+            dealt = held(name, [P, PACK * R], BF16, tag=tag)
+            engine_copy(
+                out=dealt[:].rearrange("p (t m j) -> p m t j", t=PACK, j=PACK),
+                in_=raw[:].rearrange("p j (m t) -> p m t j", t=PACK),
+            )
+            return dealt
+
+        def quantize(src, codes, scales):
+            nc.vector.quantize_mx(out=codes.bitcast(FP8X4), scales=scales, in_=src)
+
+        w1_c = [held("w1_c%d" % a, [P, R], U32) for a in range(2)]
+        w1_s = [held("w1_s%d" % a, [P, R], U8) for a in range(2)]
+        w2_c = held("w2_c", [P, H], U32)
+        w2_s = held("w2_s", [P, H], U8)
+        w1_b0 = deal(nc.scalar.copy, w1_raw[0], "w1_b0", "w1_b0")
+        w1_b1 = deal(nc.vector.tensor_copy, w1_raw[1], "w1_b1", "w1_b1")
+        quantize(w1_b0[:], w1_c[0][:], w1_s[0][:])
+        quantize(w1_b1[:], w1_c[1][:], w1_s[1][:])
+        w2_b = deal(nc.vector.tensor_copy, w2_raw, "w2_b", "w2_b")
+
+        def stage1(col):
+            acc = bank("acc1", [P, PACK, CH], 2)
+            for a in range(2):
+                for t in range(PACK):
+                    nc.tensor.matmul_mx(
+                        out=acc[:, t, :],
+                        lhsT=w1_c[a][:, t * P : (t + 1) * P].bitcast(FP8X4),
+                        lhsT_scale=w1_s[a][:, t * P : (t + 1) * P],
+                        rhs=v_w[a][:, col : col + CH].bitcast(FP8X4),
+                        rhs_scale=v_s[4 * a : P, col : col + CH],
+                        start=(a == 0 and t == 0),
+                        stop=(a == 1 and t == PACK - 1),
+                    )
+            return acc
+
+        def act_by_vector(q):
+            th = ringed("th", [P, QN, PACK], F32)
+            ab = ringed("ab", [P, QN, PACK], BF16)
+            for c in range(QN // CH):
+                acc = stage1(q * QN + c * CH)
+                cols = slice(c * CH, (c + 1) * CH)
+                nc.scalar.activation(out=th[:, cols, :], in_=acc[:].rearrange("p t n -> p n t"), func=ACT.Tanh)
+                nc.vector.tensor_tensor(
+                    out=ab[:, cols, :], in0=th[:, cols, :],
+                    in1=tg[:].unsqueeze(1).to_broadcast([P, CH, PACK]), op=ALU.mult,
+                )
+            return ab
+
+        def act_by_scalar(q):
+            th = ringed("th", [P, PACK, QN], F32)
+            sc = ringed("sc", [P, PACK, QN], BF16)
+            ab = ringed("ab", [P, QN, PACK], BF16)
+            for c in range(QN // CH):
+                acc = stage1(q * QN + c * CH)
+                nc.scalar.activation(out=th[:, :, c * CH : (c + 1) * CH], in_=acc[:], func=ACT.Tanh)
+            for t in range(PACK):
+                nc.scalar.activation(out=sc[:, t, :], in_=th[:, t, :], func=ACT.Copy, scale=tg[:, t : t + 1])
+            nc.scalar.copy(
+                out=ab[:].rearrange("p (c i) t -> p c t i", i=4),
+                in_=sc[:].rearrange("p t (c i) -> p c t i", i=4),
+            )
+            return ab
+
+        def quantize_act(ab):
+            codes = ringed("act_c", [P, QN], U32)
+            scales = ringed("act_s", [P, QN], U8)
+            quantize(ab[:].rearrange("p n t -> p (n t)"), codes[:], scales[:])
+            return codes, scales
+
+        def stage2(q, pair, act):
+            acc = bank("acc2_%d" % pair, [P, 2, QN], 1)
+            cols = slice(q * QN, (q + 1) * QN)
+            for u in range(2):
+                t = 2 * pair + u
+                for a in range(2):
+                    nc.tensor.matmul_mx(
+                        out=acc[:, u, :],
+                        lhsT=w3_d[:, a, 2 * t * P : 2 * (t + 1) * P].bitcast(FP4X4),
+                        lhsT_scale=w3s_d[:, a, t * P : (t + 1) * P],
+                        rhs=v_w[a][:, cols].bitcast(FP8X4),
+                        rhs_scale=(v_s, v_s1)[a][:, cols],
+                        start=(u == 0 and a == 0),
+                        stop=False,
+                    )
+            for u in range(2):
+                t = 2 * pair + u
+                nc.tensor.matmul_mx(
+                    out=acc[:, u, :],
+                    lhsT=w2_c[:, t * P : (t + 1) * P].bitcast(FP8X4),
+                    lhsT_scale=w2_s[:, t * P : (t + 1) * P],
+                    rhs=act[0][:].bitcast(FP8X4),
+                    rhs_scale=act[1][:],
+                    start=False,
+                    stop=(u == 1),
+                )
+            return acc
+
+        def put(q, pair, acc):
+            hs = ringed("hs", [P, 2, QN], F32, bufs=4)
+            nc.scalar.copy(out=hs[:], in_=acc[:])
+            for u in range(2):
+                t = 2 * pair + u
+                nc.vector.tensor_tensor(
+                    page[t][:].indirect(idx3[:, q * QN // 16 : (q + 1) * QN // 16]),
+                    hs[:, u, :], wg[:, t, q * QN : (q + 1) * QN], ALU.mult,
+                )
+
+        ab = act_by_vector(0)
+        quantize(w2_b[:], w2_c[:], w2_s[:])
+        act = quantize_act(ab)
+        first = stage2(0, 0, act)
+        second = stage2(0, 1, act)
+        for q in range(NQ):
+            put(q, 0, first)
+            if q + 1 < NQ:
+                act = quantize_act(act_by_scalar(q + 1))
+                first = stage2(q + 1, 0, act)
+            put(q, 1, second)
+            if q + 1 < NQ:
+                second = stage2(q + 1, 1, act)
+
+        cand_t = bank("misc", [P, P], 4)
+        nc.tensor.transpose(cand_t[:], cand_rows[:], ident[:])
+        cd = held("cd", [P, S2 // P], F32)
+        nc.scalar.copy(out=cd[:], in_=cand_t[:, 0 : S2 // P])
+
+        def against_candidates(i, codes, scales):
+            acc = bank("misc", [P, NJ], 4)
+            nc.tensor.matmul_mx(
+                out=acc[:],
+                lhsT=v2_w[:, i * P : (i + 1) * P].bitcast(FP8X4),
+                lhsT_scale=v2_s[:, i * P : (i + 1) * P],
+                rhs=codes[:].bitcast(FP8X4),
+                rhs_scale=scales[:],
+                start=True,
+                stop=True,
+            )
+            return acc
+
+        best = []
+        for i in range(S2 // P):
+            acc = against_candidates(i, qry_w, qry_s)
+            row = held("best%d" % i, [P, NJ], F32)
+            nc.scalar.activation(out=row[:], in_=acc[:], func=ACT.Identity, bias=cd[:, i : i + 1])
+            best.append(row)
+
+        x_f = held("x_f", [P, PACK, NJ], F32, tag="w1_raw0")
+        for t in range(PACK):
+            nc.vector.tensor_tensor(x_f[:, t, :], page[t][:].indirect(idx4[:]), mat_sb[:, t, :], ALU.mult)
+        x_b = held("x_b", [P, NJ, PACK], BF16, tag="w1_b0")
+        nc.vector.tensor_copy(
+            out=x_b[:].rearrange("p (c i) t -> p c t i", i=4),
+            in_=x_f[:].rearrange("p t (c i) -> p c t i", i=4),
+        )
+        x_c = held("x_c", [P, NJ], U32)
+        x_s = held("x_s", [P, NJ], U8)
+        quantize(x_b[:].rearrange("p n t -> p (n t)"), x_c[:], x_s[:])
+        for i in range(S2 // P):
+            acc = against_candidates(i, x_c, x_s)
+            nc.vector.scalar_tensor_tensor(
+                out=best[i][:], in0=acc[:], scalar=cd[:, i : i + 1], in1=best[i][:], op0=ALU.add, op1=ALU.max
+            )
+            nc.sync.dma_start(out=out[i * P : (i + 1) * P, :], in_=best[i][:])

@@ -89,19 +89,20 @@ def tile_list_mailbox_suggestion_scores_kernel(
                 in_=tab_scales[:, 4 * quad : 4 * quad + 4, :].bitcast(I32),
             )
 
+        for quad in range(4):
+            nc.gpsimd.dma_start(
+                out=w3s_raw[QUAD * quad : QUAD * quad + 4, :, :].bitcast(I32),
+                in_=w3_scales[:, 4 * quad : 4 * quad + 4, :].rearrange("a r c -> r a c").bitcast(I32),
+            )
+
+        nc.sync.dma_start(out=w3_raw[:].bitcast(I32), in_=w3_words.rearrange("a p b -> p a b").bitcast(I32))
         nc.sync.dma_start(idx2[:], offs2)
         nc.sync.dma_start(out=tab2_w[:].bitcast(I32), in_=words_of(tab2_words[0]))
         nc.sync.dma_start(out=wgs_raw[:], in_=wgs)
         nc.sync.dma_start(out=gn[:], in_=gain.rearrange("(p t) -> p t", t=PACK))
-        nc.sync.dma_start(out=w3_raw[:].bitcast(I32), in_=w3_words.rearrange("a p b -> p a b").bitcast(I32))
         nc.sync.dma_start(idx[:], offs)
         for a in range(2):
             nc.sync.dma_start(out=tab_w[a][:].bitcast(I32), in_=words_of(tab_words[a]))
-        for quad in range(4):
-            nc.sync.dma_start(
-                out=w3s_raw[QUAD * quad : QUAD * quad + 4, :, :].bitcast(I32),
-                in_=w3_scales[:, 4 * quad : 4 * quad + 4, :].rearrange("a r c -> r a c").bitcast(I32),
-            )
         nc.sync.dma_start(out=tg[:], in_=tgain.rearrange("(p t) -> p t", t=PACK))
         for a in range(2):
             nc.sync.dma_start(
@@ -124,28 +125,25 @@ def tile_list_mailbox_suggestion_scores_kernel(
 
         v2_w = held("v2_w", [P, S2], U32)
         v2_s = held("v2_s", [P, S2], U8)
-        v_w = [held("v_w%d" % a, [P, S], U32) for a in range(2)]
+        v_w = [None, None]
         v_s = held("v_s", [P, S], U8)
         w3_d = held("w3_d", [P, 2, 2 * H], U8)
-        w3s_d = held("w3s_d", [P, 2, H], U8)
+        nc.vector.tensor_copy(
+            out=w3_d[:].bitcast(U16).rearrange("p a (t m) -> p a t m", t=PACK),
+            in_=w3_raw[:].bitcast(U16).rearrange("p a (m t) -> p a t m", t=PACK),
+        )
         nc.vector.tensor_copy(v2_w[:], tab2_w[:].indirect(idx2[:]))
+        nc.vector.tensor_copy(v2_s[:], tab2_s[:].indirect(idx2[:]))
+        v_w[0] = held("v_w0", [P, S], U32, tag="tab2_s")
+        nc.vector.tensor_copy(v_w[0][:], tab_w[0][:].indirect(idx[:]))
         nc.vector.tensor_copy(v_s[:], tab_s[:].indirect(idx[:]))
         for quad in range(4):
             nc.gpsimd.dma_start(
                 out=v_s1[QUAD * quad : QUAD * quad + 4, :].bitcast(I32),
                 in_=v_s[QUAD * quad + 4 : QUAD * quad + 8, :].bitcast(I32),
             )
-        for a in range(2):
-            nc.vector.tensor_copy(v_w[a][:], tab_w[a][:].indirect(idx[:]))
-        nc.vector.tensor_copy(v2_s[:], tab2_s[:].indirect(idx2[:]))
-        nc.vector.tensor_copy(
-            out=w3_d[:].bitcast(U16).rearrange("p a (t m) -> p a t m", t=PACK),
-            in_=w3_raw[:].bitcast(U16).rearrange("p a (m t) -> p a t m", t=PACK),
-        )
-        nc.vector.tensor_copy(
-            out=w3s_d[:].rearrange("p a (t m) -> p a t m", t=PACK),
-            in_=w3s_raw[:].rearrange("p a (m t) -> p a t m", t=PACK),
-        )
+        v_w[1] = held("v_w1", [P, S], U32, tag="tab_s")
+        nc.vector.tensor_copy(v_w[1][:], tab_w[1][:].indirect(idx[:]))
 
         wg = held("wg", [P, PACK, S], F32)
         for half in range(2):
@@ -181,18 +179,24 @@ def tile_list_mailbox_suggestion_scores_kernel(
         def quantize(src, codes, scales):
             nc.vector.quantize_mx(out=codes.bitcast(FP8X4), scales=scales, in_=src)
 
-        w1_c = [held("w1_c%d" % a, [P, R], U32) for a in range(2)]
+        w1_c = [None, held("w1_c1", [P, R], U32)]
         w1_s = [held("w1_s%d" % a, [P, R], U8) for a in range(2)]
         w2_c = held("w2_c", [P, H], U32)
         w2_s = held("w2_s", [P, H], U8)
         w1_b0 = deal(nc.scalar.copy, w1_raw[0], "w1_b0", "w1_b0")
-        w1_b1 = deal(nc.vector.tensor_copy, w1_raw[1], "w1_b1", "w1_b1")
+        w1_b1 = deal(nc.vector.tensor_copy, w1_raw[1], "w1_b1", "tab_w1")
+        w1_c[0] = held("w1_c0", [P, R], U32, tag="w1_raw1")
         quantize(w1_b0[:], w1_c[0][:], w1_s[0][:])
         quantize(w1_b1[:], w1_c[1][:], w1_s[1][:])
-        w2_b = deal(nc.vector.tensor_copy, w2_raw, "w2_b", "w2_b")
+        w3s_d = held("w3s_d", [P, 2, H], U8, tag="w1_b0")
+        nc.vector.tensor_copy(
+            out=w3s_d[:].rearrange("p a (t m) -> p a t m", t=PACK),
+            in_=w3s_raw[:].rearrange("p a (m t) -> p a t m", t=PACK),
+        )
+        w2_b = deal(nc.vector.tensor_copy, w2_raw, "w2_b", "w3s_raw")
 
-        def stage1(col):
-            acc = bank("acc1", [P, PACK, CH], 2)
+        def stage1(col, tag, bufs):
+            acc = bank(tag, [P, PACK, CH], bufs)
             for a in range(2):
                 for t in range(PACK):
                     nc.tensor.matmul_mx(
@@ -207,10 +211,10 @@ def tile_list_mailbox_suggestion_scores_kernel(
             return acc
 
         def act_by_vector(q):
-            th = ringed("th", [P, QN, PACK], F32)
+            th = held("th_first", [P, QN, PACK], F32)
             ab = ringed("ab", [P, QN, PACK], BF16)
             for c in range(QN // CH):
-                acc = stage1(q * QN + c * CH)
+                acc = stage1(q * QN + c * CH, "acc1", 2)
                 cols = slice(c * CH, (c + 1) * CH)
                 nc.scalar.activation(out=th[:, cols, :], in_=acc[:].rearrange("p t n -> p n t"), func=ACT.Tanh)
                 nc.vector.tensor_tensor(
@@ -220,18 +224,18 @@ def tile_list_mailbox_suggestion_scores_kernel(
             return ab
 
         def act_by_scalar(q):
-            th = ringed("th", [P, PACK, QN], F32)
-            sc = ringed("sc", [P, PACK, QN], BF16)
             ab = ringed("ab", [P, QN, PACK], BF16)
             for c in range(QN // CH):
-                acc = stage1(q * QN + c * CH)
-                nc.scalar.activation(out=th[:, :, c * CH : (c + 1) * CH], in_=acc[:], func=ACT.Tanh)
-            for t in range(PACK):
-                nc.scalar.activation(out=sc[:, t, :], in_=th[:, t, :], func=ACT.Copy, scale=tg[:, t : t + 1])
-            nc.scalar.copy(
-                out=ab[:].rearrange("p (c i) t -> p c t i", i=4),
-                in_=sc[:].rearrange("p t (c i) -> p c t i", i=4),
-            )
+                acc = stage1(q * QN + c * CH, "acc1", 2) if c == 0 else stage1(q * QN + c * CH, "acc2_0", 1)
+                th = ringed("th", [P, PACK, CH], F32, bufs=1)
+                nc.scalar.activation(out=th[:], in_=acc[:], func=ACT.Tanh)
+                sc = held("sc", [P, PACK, CH], BF16, tag="turn%d_%d" % (c, (q + c) % 2))
+                for t in range(PACK):
+                    nc.scalar.activation(out=sc[:, t, :], in_=th[:, t, :], func=ACT.Copy, scale=tg[:, t : t + 1])
+                nc.scalar.copy(
+                    out=ab[:, c * CH : (c + 1) * CH, :].rearrange("p (c i) t -> p c t i", i=4),
+                    in_=sc[:].rearrange("p t (c i) -> p c t i", i=4),
+                )
             return ab
 
         def quantize_act(ab):
@@ -243,9 +247,9 @@ def tile_list_mailbox_suggestion_scores_kernel(
         def stage2(q, pair, act):
             acc = bank("acc2_%d" % pair, [P, 2, QN], 1)
             cols = slice(q * QN, (q + 1) * QN)
-            for u in range(2):
-                t = 2 * pair + u
-                for a in range(2):
+            for a in range(2):
+                for u in range(2):
+                    t = 2 * pair + u
                     nc.tensor.matmul_mx(
                         out=acc[:, u, :],
                         lhsT=w3_d[:, a, 2 * t * P : 2 * (t + 1) * P].bitcast(FP4X4),
@@ -269,7 +273,7 @@ def tile_list_mailbox_suggestion_scores_kernel(
             return acc
 
         def put(q, pair, acc):
-            hs = ringed("hs", [P, 2, QN], F32, bufs=4)
+            hs = held("hs", [P, 2, QN], F32, tag="turn%d_%d" % (pair, q % 2))
             nc.scalar.copy(out=hs[:], in_=acc[:])
             for u in range(2):
                 t = 2 * pair + u
@@ -292,13 +296,13 @@ def tile_list_mailbox_suggestion_scores_kernel(
             if q + 1 < NQ:
                 second = stage2(q + 1, 1, act)
 
-        cand_t = bank("misc", [P, P], 4)
+        cand_t = bank("acc1", [P, P], 2)
         nc.tensor.transpose(cand_t[:], cand_rows[:], ident[:])
         cd = held("cd", [P, S2 // P], F32)
         nc.scalar.copy(out=cd[:], in_=cand_t[:, 0 : S2 // P])
 
-        def against_candidates(i, codes, scales):
-            acc = bank("misc", [P, NJ], 4)
+        def against_candidates(i, codes, scales, tag, bufs):
+            acc = bank(tag, [P, NJ], bufs)
             nc.tensor.matmul_mx(
                 out=acc[:],
                 lhsT=v2_w[:, i * P : (i + 1) * P].bitcast(FP8X4),
@@ -312,7 +316,7 @@ def tile_list_mailbox_suggestion_scores_kernel(
 
         best = []
         for i in range(S2 // P):
-            acc = against_candidates(i, qry_w, qry_s)
+            acc = against_candidates(i, qry_w, qry_s, "acc1", 2)
             row = held("best%d" % i, [P, NJ], F32)
             nc.scalar.activation(out=row[:], in_=acc[:], func=ACT.Identity, bias=cd[:, i : i + 1])
             best.append(row)
@@ -320,7 +324,7 @@ def tile_list_mailbox_suggestion_scores_kernel(
         x_f = held("x_f", [P, PACK, NJ], F32, tag="w1_raw0")
         for t in range(PACK):
             nc.vector.tensor_tensor(x_f[:, t, :], page[t][:].indirect(idx4[:]), mat_sb[:, t, :], ALU.mult)
-        x_b = held("x_b", [P, NJ, PACK], BF16, tag="w1_b0")
+        x_b = held("x_b", [P, NJ, PACK], BF16, tag="tab_w1")
         nc.vector.tensor_copy(
             out=x_b[:].rearrange("p (c i) t -> p c t i", i=4),
             in_=x_f[:].rearrange("p t (c i) -> p c t i", i=4),
@@ -329,7 +333,7 @@ def tile_list_mailbox_suggestion_scores_kernel(
         x_s = held("x_s", [P, NJ], U8)
         quantize(x_b[:].rearrange("p n t -> p (n t)"), x_c[:], x_s[:])
         for i in range(S2 // P):
-            acc = against_candidates(i, x_c, x_s)
+            acc = against_candidates(i, x_c, x_s, "misc", 4)
             nc.vector.scalar_tensor_tensor(
                 out=best[i][:], in0=acc[:], scalar=cd[:, i : i + 1], in1=best[i][:], op0=ALU.add, op1=ALU.max
             )

@@ -24,6 +24,7 @@ QUAD = 32
 QN = 256
 NQ = S // QN
 CH = 128
+QUADS = (0, 2, 1, 3)
 
 
 def tile_list_mailbox_suggestion_scores_kernel(
@@ -61,190 +62,194 @@ def tile_list_mailbox_suggestion_scores_kernel(
         w3_raw = held("w3_raw", [P, 2, 2 * H], U8)
         w3s_raw = held("w3s_raw", [P, 2, H], U8)
         v_s1 = held("v_s1", [P, S], U8)
-        qry_w = held("qry_w", [P, NJ], U32)
-        qry_s = held("qry_s", [P, NJ], U8)
-        cand_rows = held("cand_rows", [P, P], F32)
         ident = held("ident", [P, P], F32)
         wgs_raw = held("wgs_raw", [P, S], F32)
         tg = held("tg", [P, PACK], F32)
         gn = held("gn", [P, PACK], F32)
         w1_raw = [held("w1_raw%d" % a, [P, PACK, R], F32) for a in range(2)]
-        w2_raw = held("w2_raw", [P, PACK, H], F32)
-        page = [held("page%d" % t, [P, T2], F32) for t in range(PACK)]
-        mat_sb = held("mat_sb", [P, PACK, NJ], F32)
 
-        for plane in (tab2_s, tab_s, w3s_raw, v_s1, qry_s):
+        nc.gpsimd.memset(tab2_s[:].bitcast(I32), 0)
+        for plane in (tab_s, w3s_raw, v_s1):
             nc.vector.memset(plane[:].bitcast(I32), 0)
-        nc.vector.memset(cand_rows[:], 0.0)
         make_identity(nc, ident[:])
-
-        for quad in range(4):
-            nc.gpsimd.dma_start(
-                out=tab2_s[QUAD * quad : QUAD * quad + 4, :].bitcast(I32),
-                in_=tab2_scales[0, 4 * quad : 4 * quad + 4, :].bitcast(I32),
-            )
-        for quad in range(4):
-            nc.gpsimd.dma_start(
-                out=tab_s[QUAD * quad : QUAD * quad + 8, :].bitcast(I32),
-                in_=tab_scales[:, 4 * quad : 4 * quad + 4, :].bitcast(I32),
-            )
-
-        for quad in range(4):
+        nc.gpsimd.dma_start(out=gn[:], in_=gain.rearrange("(p t) -> p t", t=PACK))
+        for quad in QUADS:
             nc.gpsimd.dma_start(
                 out=w3s_raw[QUAD * quad : QUAD * quad + 4, :, :].bitcast(I32),
                 in_=w3_scales[:, 4 * quad : 4 * quad + 4, :].rearrange("a r c -> r a c").bitcast(I32),
             )
+        nc.gpsimd.dma_start(out=tg[:], in_=tgain.rearrange("(p t) -> p t", t=PACK))
 
-        nc.sync.dma_start(out=w3_raw[:].bitcast(I32), in_=w3_words.rearrange("a p b -> p a b").bitcast(I32))
-        nc.sync.dma_start(idx2[:], offs2)
         nc.sync.dma_start(out=tab2_w[:].bitcast(I32), in_=words_of(tab2_words[0]))
+        nc.sync.dma_start(idx2[:], offs2)
+        for quad in QUADS:
+            nc.sync.dma_start(
+                out=tab2_s[QUAD * quad : QUAD * quad + 4, :].bitcast(I32),
+                in_=tab2_scales[0, 4 * quad : 4 * quad + 4, :].bitcast(I32),
+            )
         nc.sync.dma_start(out=wgs_raw[:], in_=wgs)
-        nc.sync.dma_start(out=gn[:], in_=gain.rearrange("(p t) -> p t", t=PACK))
+        nc.sync.dma_start(out=tab_w[0][:].bitcast(I32), in_=words_of(tab_words[0]))
         nc.sync.dma_start(idx[:], offs)
-        for a in range(2):
-            nc.sync.dma_start(out=tab_w[a][:].bitcast(I32), in_=words_of(tab_words[a]))
-        nc.sync.dma_start(out=tg[:], in_=tgain.rearrange("(p t) -> p t", t=PACK))
-        for a in range(2):
+        for quad in QUADS:
             nc.sync.dma_start(
-                out=w1_raw[a][:], in_=w1[a * PASS : (a + 1) * PASS, :].rearrange("(p j) c -> p j c", j=PACK)
+                out=tab_s[QUAD * quad : QUAD * quad + 8, :].bitcast(I32),
+                in_=tab_scales[:, 4 * quad : 4 * quad + 4, :].bitcast(I32),
             )
+        w1_rows = w1.rearrange("(a p j) c -> a p j c", a=2, j=PACK)
+        nc.sync.dma_start(out=w1_raw[0][:], in_=w1_rows[0])
+        nc.sync.dma_start(out=w1_raw[1][:], in_=w1_rows[1])
+        nc.sync.dma_start(out=w3_raw[:].bitcast(I32), in_=w3_words.rearrange("a p b -> p a b").bitcast(I32))
         nc.sync.dma_start(idx3[:], offs3)
-        nc.sync.dma_start(out=w2_raw[:], in_=w2.rearrange("(p j) c -> p j c", j=PACK))
-        page_rows = page0.rearrange("(p t) s -> p t s", t=PACK)
-        for t in range(PACK):
-            nc.sync.dma_start(out=page[t][:], in_=page_rows[:, t, :])
-        nc.sync.dma_start(out=qry_w[:].bitcast(I32), in_=words_of(qry_words[0]))
-        for quad in range(4):
-            nc.sync.dma_start(
-                out=qry_s[QUAD * quad : QUAD * quad + 4, :].bitcast(I32),
-                in_=qry_scales[0, 4 * quad : 4 * quad + 4, :].bitcast(I32),
-            )
-        nc.sync.dma_start(out=cand_rows[0 : S2 // P, :], in_=cand.rearrange("(i p) -> i p", p=P))
+        nc.sync.dma_start(out=tab_w[1][:].bitcast(I32), in_=words_of(tab_words[1]))
         nc.sync.dma_start(idx4[:], offs4)
-        nc.sync.dma_start(out=mat_sb[:], in_=mat.rearrange("(p t) j -> p t j", t=PACK))
 
         v2_w = held("v2_w", [P, S2], U32)
         v2_s = held("v2_s", [P, S2], U8)
-        v_w = [None, None]
+        v_w0 = held("v_w0", [P, S], U32)
         v_s = held("v_s", [P, S], U8)
-        w3_d = held("w3_d", [P, 2, 2 * H], U8)
-        nc.vector.tensor_copy(
-            out=w3_d[:].bitcast(U16).rearrange("p a (t m) -> p a t m", t=PACK),
-            in_=w3_raw[:].bitcast(U16).rearrange("p a (m t) -> p a t m", t=PACK),
-        )
         nc.vector.tensor_copy(v2_w[:], tab2_w[:].indirect(idx2[:]))
         nc.vector.tensor_copy(v2_s[:], tab2_s[:].indirect(idx2[:]))
-        v_w[0] = held("v_w0", [P, S], U32, tag="tab2_s")
-        nc.vector.tensor_copy(v_w[0][:], tab_w[0][:].indirect(idx[:]))
+        nc.vector.tensor_copy(v_w0[:], tab_w[0][:].indirect(idx[:]))
+        w2_raw = held("w2_raw", [P, PACK, H], F32, tag="tab_w0")
+        nc.sync.dma_start(out=w2_raw[:], in_=w2.rearrange("(p j) c -> p j c", j=PACK))
         nc.vector.tensor_copy(v_s[:], tab_s[:].indirect(idx[:]))
-        for quad in range(4):
-            nc.gpsimd.dma_start(
+        for quad in QUADS:
+            nc.sync.dma_start(
                 out=v_s1[QUAD * quad : QUAD * quad + 4, :].bitcast(I32),
                 in_=v_s[QUAD * quad + 4 : QUAD * quad + 8, :].bitcast(I32),
             )
-        v_w[1] = held("v_w1", [P, S], U32, tag="tab_s")
-        nc.vector.tensor_copy(v_w[1][:], tab_w[1][:].indirect(idx[:]))
 
-        wg = held("wg", [P, PACK, S], F32)
+        page_rows = page0.rearrange("(p t) s -> p t s", t=PACK)
+        page = []
+
+        def load_page(tag):
+            t = len(page)
+            rows = held("page%d" % t, [P, T2], F32, tag=tag)
+            nc.sync.dma_start(out=rows[:], in_=page_rows[:, t, :])
+            page.append(rows)
+
+        load_page("tab_s")
+
+        wg = []
+        spread = []
         for half in range(2):
             turned = bank("misc", [P, 4, CH], 4)
             for c in range(4):
                 col = (4 * half + c) * CH
                 nc.tensor.transpose(turned[:, c, :], wgs_raw[:, col : col + CH], ident[:])
-            spread = []
             for c in range(4):
-                rep = ringed("rep", [P, PACK, 4, QUAD], F32, bufs=4)
+                rep = held("rep%d" % (4 * half + c), [P, PACK, 4, QUAD], F32)
                 nc.scalar.copy(
                     out=rep[:],
                     in_=turned[:, c, :].rearrange("j (m t) -> j t m", t=PACK).unsqueeze(2).to_broadcast([P, PACK, 4, QUAD]),
                 )
                 spread.append(rep)
+
+        def deal_wgs(half, tag):
+            wg.append(held("wg%d" % half, [P, PACK, S // 2], F32, tag=tag))
             for t in range(PACK):
                 back = bank("misc", [P, 4, CH], 4)
                 for c in range(4):
-                    nc.tensor.transpose(back[:, c, :], spread[c][:, t, :, :].rearrange("j q m -> j (q m)"), ident[:])
+                    nc.tensor.transpose(back[:, c, :], spread[4 * half + c][:, t, :, :].rearrange("j q m -> j (q m)"), ident[:])
                 nc.scalar.activation(
-                    out=wg[:, t, half * 512 : (half + 1) * 512], in_=back[:].rearrange("p c j -> p (c j)"),
+                    out=wg[half][:, t, :], in_=back[:].rearrange("p c j -> p (c j)"),
                     func=ACT.Copy, scale=gn[:, t : t + 1],
                 )
 
-        def deal(engine_copy, raw, name, tag):
-            dealt = held(name, [P, PACK * R], BF16, tag=tag)
+        deal_wgs(0, "wg0")
+
+        def deal(engine_copy, raw, name, t0, t1, tag=None):
+            dealt = held(name, [P, (t1 - t0) * R], BF16, tag=tag)
             engine_copy(
-                out=dealt[:].rearrange("p (t m j) -> p m t j", t=PACK, j=PACK),
-                in_=raw[:].rearrange("p j (m t) -> p m t j", t=PACK),
+                out=dealt[:].rearrange("p (t m j) -> p m t j", m=P, j=PACK),
+                in_=raw[:].rearrange("p j (m t) -> p m t j", t=PACK)[:, :, t0:t1, :],
             )
             return dealt
 
         def quantize(src, codes, scales):
             nc.vector.quantize_mx(out=codes.bitcast(FP8X4), scales=scales, in_=src)
 
-        w1_c = [None, held("w1_c1", [P, R], U32)]
+        w1_c = [held("w1_c0", [P, R], U32)]
         w1_s = [held("w1_s%d" % a, [P, R], U8) for a in range(2)]
-        w2_c = held("w2_c", [P, H], U32)
-        w2_s = held("w2_s", [P, H], U8)
-        w1_b0 = deal(nc.scalar.copy, w1_raw[0], "w1_b0", "w1_b0")
-        w1_b1 = deal(nc.vector.tensor_copy, w1_raw[1], "w1_b1", "tab_w1")
-        w1_c[0] = held("w1_c0", [P, R], U32, tag="w1_raw1")
+        w2_c = [held("w2_c%d" % pair, [P, 2 * P], U32) for pair in range(2)]
+        w2_s = [held("w2_s%d" % pair, [P, 2 * P], U8) for pair in range(2)]
+        w1_b0 = deal(nc.scalar.copy, w1_raw[0], "w1_b0", 0, PACK)
+        deal_wgs(1, "w1_raw0")
+        w1_b1 = deal(nc.vector.tensor_copy, w1_raw[1], "w1_b1", 0, PACK)
+        load_page("w1_raw1")
+        w3_d = held("w3_d", [P, 2, 2 * H], U8)
+        nc.vector.tensor_copy(
+            out=w3_d[:].bitcast(U16).rearrange("p a (t m) -> p a t m", t=PACK),
+            in_=w3_raw[:].bitcast(U16).rearrange("p a (m t) -> p a t m", t=PACK),
+        )
+        load_page("w3_raw")
         quantize(w1_b0[:], w1_c[0][:], w1_s[0][:])
+        w1_c.append(held("w1_c1", [P, R], U32, tag="w1_b0"))
         quantize(w1_b1[:], w1_c[1][:], w1_s[1][:])
-        w3s_d = held("w3s_d", [P, 2, H], U8, tag="w1_b0")
+        w3s_d = held("w3s_d", [P, 2, H], U8, tag="w1_b1")
         nc.vector.tensor_copy(
             out=w3s_d[:].rearrange("p a (t m) -> p a t m", t=PACK),
             in_=w3s_raw[:].rearrange("p a (m t) -> p a t m", t=PACK),
         )
-        w2_b = deal(nc.vector.tensor_copy, w2_raw, "w2_b", "w3s_raw")
+        v_w1 = held("v_w1", [P, S], U32, tag="w3s_raw")
+        for half in range(2):
+            nc.vector.tensor_copy(
+                v_w1[:, half * S // 2 : (half + 1) * S // 2],
+                tab_w[1][:].indirect(idx[:, half * S // 32 : (half + 1) * S // 32]),
+            )
+        load_page("tab_w1")
+        v_w = (v_w0, v_w1)
 
-        def stage1(col, tag, bufs):
-            acc = bank(tag, [P, PACK, CH], bufs)
+        def stage1(slices, col, n, tag="acc1", bufs=2):
+            acc = bank(tag, [P, len(slices), n], bufs)
             for a in range(2):
-                for t in range(PACK):
+                for u, t in enumerate(slices):
                     nc.tensor.matmul_mx(
-                        out=acc[:, t, :],
+                        out=acc[:, u, :],
                         lhsT=w1_c[a][:, t * P : (t + 1) * P].bitcast(FP8X4),
                         lhsT_scale=w1_s[a][:, t * P : (t + 1) * P],
-                        rhs=v_w[a][:, col : col + CH].bitcast(FP8X4),
-                        rhs_scale=v_s[4 * a : P, col : col + CH],
-                        start=(a == 0 and t == 0),
-                        stop=(a == 1 and t == PACK - 1),
+                        rhs=v_w[a][:, col : col + n].bitcast(FP8X4),
+                        rhs_scale=v_s[4 * a : P, col : col + n],
+                        start=(a == 0 and u == 0),
+                        stop=(a == 1 and u == len(slices) - 1),
                     )
             return acc
 
-        def act_by_vector(q):
+        def act_by_vector():
             th = held("th_first", [P, QN, PACK], F32)
-            ab = ringed("ab", [P, QN, PACK], BF16)
-            for c in range(QN // CH):
-                acc = stage1(q * QN + c * CH, "acc1", 2)
-                cols = slice(c * CH, (c + 1) * CH)
+            ab = held("ab_first", [P, QN, PACK], BF16, tag="w2_b0")
+            codes, scales = held("act_c_first", [P, QN], U32), held("act_s_first", [P, QN], U8)
+            chunks = [slice(c * CH, (c + 1) * CH) for c in range(QN // CH)]
+            for cols in chunks:
+                acc = stage1(range(PACK), cols.start, CH)
                 nc.scalar.activation(out=th[:, cols, :], in_=acc[:].rearrange("p t n -> p n t"), func=ACT.Tanh)
                 nc.vector.tensor_tensor(
                     out=ab[:, cols, :], in0=th[:, cols, :],
                     in1=tg[:].unsqueeze(1).to_broadcast([P, CH, PACK]), op=ALU.mult,
                 )
-            return ab
+            for cols in chunks:
+                quantize(ab[:, cols, :].rearrange("p n t -> p (n t)"), codes[:, cols], scales[:, cols])
+            return codes, scales, chunks
 
         def act_by_scalar(q):
+            th = ringed("th", [P, PACK, QN], F32, bufs=1)
+            sc = held("sc", [P, PACK, QN], BF16, tag="turn%d" % ((q + 1) % 2))
             ab = ringed("ab", [P, QN, PACK], BF16)
-            for c in range(QN // CH):
-                acc = stage1(q * QN + c * CH, "acc1", 2) if c == 0 else stage1(q * QN + c * CH, "acc2_0", 1)
-                th = ringed("th", [P, PACK, CH], F32, bufs=1)
-                nc.scalar.activation(out=th[:], in_=acc[:], func=ACT.Tanh)
-                sc = held("sc", [P, PACK, CH], BF16, tag="turn%d_%d" % (c, (q + c) % 2))
-                for t in range(PACK):
-                    nc.scalar.activation(out=sc[:, t, :], in_=th[:, t, :], func=ACT.Copy, scale=tg[:, t : t + 1])
-                nc.scalar.copy(
-                    out=ab[:, c * CH : (c + 1) * CH, :].rearrange("p (c i) t -> p c t i", i=4),
-                    in_=sc[:].rearrange("p t (c i) -> p c t i", i=4),
-                )
-            return ab
-
-        def quantize_act(ab):
-            codes = ringed("act_c", [P, QN], U32)
-            scales = ringed("act_s", [P, QN], U8)
+            codes, scales = ringed("act_c", [P, QN], U32), ringed("act_s", [P, QN], U8)
+            for pair in range(2):
+                acc = stage1((0, 1), q * QN, QN) if pair == 0 else stage1((2, 3), q * QN, QN, "acc2_0", 1)
+                nc.scalar.activation(out=th[:, 2 * pair : 2 * pair + 2, :], in_=acc[:], func=ACT.Tanh)
+            for t in range(PACK):
+                nc.scalar.activation(out=sc[:, t, :], in_=th[:, t, :], func=ACT.Copy, scale=tg[:, t : t + 1])
+            nc.scalar.copy(
+                out=ab[:].rearrange("p (c i) t -> p c t i", i=4),
+                in_=sc[:].rearrange("p t (c i) -> p c t i", i=4),
+            )
             quantize(ab[:].rearrange("p n t -> p (n t)"), codes[:], scales[:])
-            return codes, scales
+            return codes, scales, [slice(0, QN)]
 
         def stage2(q, pair, act):
+            codes, scales, chunks = act
             acc = bank("acc2_%d" % pair, [P, 2, QN], 1)
             cols = slice(q * QN, (q + 1) * QN)
             for a in range(2):
@@ -259,38 +264,57 @@ def tile_list_mailbox_suggestion_scores_kernel(
                         start=(u == 0 and a == 0),
                         stop=False,
                     )
-            for u in range(2):
-                t = 2 * pair + u
-                nc.tensor.matmul_mx(
-                    out=acc[:, u, :],
-                    lhsT=w2_c[:, t * P : (t + 1) * P].bitcast(FP8X4),
-                    lhsT_scale=w2_s[:, t * P : (t + 1) * P],
-                    rhs=act[0][:].bitcast(FP8X4),
-                    rhs_scale=act[1][:],
-                    start=False,
-                    stop=(u == 1),
-                )
+            for part in chunks:
+                for u in range(2):
+                    nc.tensor.matmul_mx(
+                        out=acc[:, u, part],
+                        lhsT=w2_c[pair][:, u * P : (u + 1) * P].bitcast(FP8X4),
+                        lhsT_scale=w2_s[pair][:, u * P : (u + 1) * P],
+                        rhs=codes[:, part].bitcast(FP8X4),
+                        rhs_scale=scales[:, part],
+                        start=False,
+                        stop=(u == 1 and part.stop == QN),
+                    )
             return acc
 
         def put(q, pair, acc):
-            hs = held("hs", [P, 2, QN], F32, tag="turn%d_%d" % (pair, q % 2))
+            hs = held("hs", [P, 2, QN], F32, tag=("hs%d", "turn%d")[pair] % (q % 2))
             nc.scalar.copy(out=hs[:], in_=acc[:])
             for u in range(2):
                 t = 2 * pair + u
                 nc.vector.tensor_tensor(
                     page[t][:].indirect(idx3[:, q * QN // 16 : (q + 1) * QN // 16]),
-                    hs[:, u, :], wg[:, t, q * QN : (q + 1) * QN], ALU.mult,
+                    hs[:, u, :], wg[q // 2][:, t, (q % 2) * QN : (q % 2 + 1) * QN], ALU.mult,
                 )
 
-        ab = act_by_vector(0)
-        quantize(w2_b[:], w2_c[:], w2_s[:])
-        act = quantize_act(ab)
+        w2_b0 = deal(nc.vector.tensor_copy, w2_raw, "w2_b0", 0, 2)
+        quantize(w2_b0[:], w2_c[0][:], w2_s[0][:])
+        act = act_by_vector()
         first = stage2(0, 0, act)
+        w2_b1 = deal(nc.vector.tensor_copy, w2_raw, "w2_b1", 2, PACK, "th_first")
+        quantize(w2_b1[:], w2_c[1][:], w2_s[1][:])
         second = stage2(0, 1, act)
+
+        mat_sb = held("mat_sb", [P, PACK, NJ], F32, tag="tab_w0")
+        nc.sync.dma_start(out=mat_sb[:], in_=mat.rearrange("(p t) j -> p t j", t=PACK))
+        qry_w = held("qry_w", [P, NJ], U32, tag="w2_b0")
+        nc.sync.dma_start(out=qry_w[:].bitcast(I32), in_=words_of(qry_words[0]))
+        qry_s = held("qry_s", [P, NJ], U8, tag="th_first")
+        nc.gpsimd.memset(qry_s[:].bitcast(I32), 0)
+        for quad in QUADS:
+            nc.sync.dma_start(
+                out=qry_s[QUAD * quad : QUAD * quad + 4, :].bitcast(I32),
+                in_=qry_scales[0, 4 * quad : 4 * quad + 4, :].bitcast(I32),
+            )
+
+        cand_rows = held("cand_rows", [P, P], F32, tag="act_c_first")
+        nc.gpsimd.memset(cand_rows[:], 0.0)
+        nc.sync.dma_start(out=cand_rows[0 : S2 // P, :], in_=cand.rearrange("(i p) -> i p", p=P))
+
         for q in range(NQ):
             put(q, 0, first)
             if q + 1 < NQ:
-                act = quantize_act(act_by_scalar(q + 1))
+                act = act_by_scalar(q + 1)
                 first = stage2(q + 1, 0, act)
             put(q, 1, second)
             if q + 1 < NQ:
@@ -301,40 +325,51 @@ def tile_list_mailbox_suggestion_scores_kernel(
         cd = held("cd", [P, S2 // P], F32)
         nc.scalar.copy(out=cd[:], in_=cand_t[:, 0 : S2 // P])
 
-        def against_candidates(i, codes, scales, tag, bufs):
+        def against_candidates(i, codes, scales, tag, bufs, parts):
             acc = bank(tag, [P, NJ], bufs)
-            nc.tensor.matmul_mx(
-                out=acc[:],
-                lhsT=v2_w[:, i * P : (i + 1) * P].bitcast(FP8X4),
-                lhsT_scale=v2_s[:, i * P : (i + 1) * P],
-                rhs=codes[:].bitcast(FP8X4),
-                rhs_scale=scales[:],
-                start=True,
-                stop=True,
-            )
+            for part in parts:
+                nc.tensor.matmul_mx(
+                    out=acc[:, part],
+                    lhsT=v2_w[:, i * P : (i + 1) * P].bitcast(FP8X4),
+                    lhsT_scale=v2_s[:, i * P : (i + 1) * P],
+                    rhs=codes[:, part].bitcast(FP8X4),
+                    rhs_scale=scales[:, part],
+                    start=True,
+                    stop=True,
+                )
             return acc
 
+        whole = [slice(0, NJ)]
+        halves = [slice(0, NJ // 2), slice(NJ // 2, NJ)]
         best = []
         for i in range(S2 // P):
-            acc = against_candidates(i, qry_w, qry_s, "acc1", 2)
+            acc = against_candidates(i, qry_w, qry_s, "acc1", 2, whole)
             row = held("best%d" % i, [P, NJ], F32)
             nc.scalar.activation(out=row[:], in_=acc[:], func=ACT.Identity, bias=cd[:, i : i + 1])
             best.append(row)
 
-        x_f = held("x_f", [P, PACK, NJ], F32, tag="w1_raw0")
+        x_f = held("x_f", [P, PACK, NJ], F32)
         for t in range(PACK):
-            nc.vector.tensor_tensor(x_f[:, t, :], page[t][:].indirect(idx4[:]), mat_sb[:, t, :], ALU.mult)
-        x_b = held("x_b", [P, NJ, PACK], BF16, tag="tab_w1")
-        nc.vector.tensor_copy(
-            out=x_b[:].rearrange("p (c i) t -> p c t i", i=4),
-            in_=x_f[:].rearrange("p t (c i) -> p c t i", i=4),
-        )
-        x_c = held("x_c", [P, NJ], U32)
+            for part in halves if t == PACK - 1 else whole:
+                nc.vector.tensor_tensor(
+                    x_f[:, t, part], page[t][:].indirect(idx4[:, part.start // 16 : part.stop // 16]),
+                    mat_sb[:, t, part], ALU.mult,
+                )
+        x_b = held("x_b", [P, NJ, PACK], BF16)
+        x_c = held("x_c", [P, NJ], U32, tag="w2_b0")
         x_s = held("x_s", [P, NJ], U8)
-        quantize(x_b[:].rearrange("p n t -> p (n t)"), x_c[:], x_s[:])
-        for i in range(S2 // P):
-            acc = against_candidates(i, x_c, x_s, "misc", 4)
-            nc.vector.scalar_tensor_tensor(
-                out=best[i][:], in0=acc[:], scalar=cd[:, i : i + 1], in1=best[i][:], op0=ALU.add, op1=ALU.max
+        for part in halves:
+            nc.vector.tensor_copy(
+                out=x_b[:, part, :].rearrange("p (c i) t -> p c t i", i=4),
+                in_=x_f[:, :, part].rearrange("p t (c i) -> p c t i", i=4),
             )
-            nc.sync.dma_start(out=out[i * P : (i + 1) * P, :], in_=best[i][:])
+        for part in halves:
+            quantize(x_b[:, part, :].rearrange("p n t -> p (n t)"), x_c[:, part], x_s[:, part])
+        for i in range(S2 // P):
+            acc = against_candidates(i, x_c, x_s, "misc", 4, halves if i == 0 else whole)
+            for part in halves if i == S2 // P - 1 else whole:
+                nc.vector.scalar_tensor_tensor(
+                    out=best[i][:, part], in0=acc[:, part], scalar=cd[:, i : i + 1], in1=best[i][:, part],
+                    op0=ALU.add, op1=ALU.max,
+                )
+                nc.sync.dma_start(out=out[i * P : (i + 1) * P, part], in_=best[i][:, part])

@@ -84,7 +84,7 @@ def tile_list_mailbox_suggestion_scores_kernel(
         nc.sync.dma_start(idx2[:], offs2)
         for quad in QUADS:
             nc.sync.dma_start(
-                out=tab2_s[QUAD * quad : QUAD * quad + 4, :].bitcast(I32),
+                out=tab2_s[QUAD * quad + 8 : QUAD * quad + 12, :].bitcast(I32),
                 in_=tab2_scales[0, 4 * quad : 4 * quad + 4, :].bitcast(I32),
             )
         nc.sync.dma_start(out=wgs_raw[:], in_=wgs)
@@ -237,7 +237,7 @@ def tile_list_mailbox_suggestion_scores_kernel(
             ab = ringed("ab", [P, QN, PACK], BF16)
             codes, scales = ringed("act_c", [P, QN], U32), ringed("act_s", [P, QN], U8)
             for pair in range(2):
-                acc = stage1((0, 1), q * QN, QN) if pair == 0 else stage1((2, 3), q * QN, QN, "acc2_0", 1)
+                acc = stage1((0, 1), q * QN, QN) if pair == 0 else stage1((2, 3), q * QN, QN, *(("acc2_0", 1) if q == 1 else ("acc1", 2)))
                 nc.scalar.activation(out=th[:, 2 * pair : 2 * pair + 2, :], in_=acc[:], func=ACT.Tanh)
             for t in range(PACK):
                 nc.scalar.activation(out=sc[:, t, :], in_=th[:, t, :], func=ACT.Copy, scale=tg[:, t : t + 1])
@@ -279,7 +279,8 @@ def tile_list_mailbox_suggestion_scores_kernel(
 
         def put(q, pair, acc):
             hs = held("hs", [P, 2, QN], F32, tag=("hs%d", "turn%d")[pair] % (q % 2))
-            nc.scalar.copy(out=hs[:], in_=acc[:])
+            for part in (slice(0, 1), slice(1, 2)) if q == 0 and pair == 0 else (slice(0, 2),):
+                nc.scalar.copy(out=hs[:, part, :], in_=acc[:, part, :])
             for u in range(2):
                 t = 2 * pair + u
                 nc.vector.tensor_tensor(
@@ -331,7 +332,7 @@ def tile_list_mailbox_suggestion_scores_kernel(
                 nc.tensor.matmul_mx(
                     out=acc[:, part],
                     lhsT=v2_w[:, i * P : (i + 1) * P].bitcast(FP8X4),
-                    lhsT_scale=v2_s[:, i * P : (i + 1) * P],
+                    lhsT_scale=v2_s[8:P, i * P : (i + 1) * P],
                     rhs=codes[:, part].bitcast(FP8X4),
                     rhs_scale=scales[:, part],
                     start=True,
@@ -366,8 +367,8 @@ def tile_list_mailbox_suggestion_scores_kernel(
         for part in halves:
             quantize(x_b[:, part, :].rearrange("p n t -> p (n t)"), x_c[:, part], x_s[:, part])
         for i in range(S2 // P):
-            acc = against_candidates(i, x_c, x_s, "misc", 4, halves if i == 0 else whole)
-            for part in halves if i == S2 // P - 1 else whole:
+            for part in halves if i in (0, S2 // P - 1) else whole:
+                acc = against_candidates(i, x_c, x_s, "misc", 4, [part])
                 nc.vector.scalar_tensor_tensor(
                     out=best[i][:, part], in0=acc[:, part], scalar=cd[:, i : i + 1], in1=best[i][:, part],
                     op0=ALU.add, op1=ALU.max,

from contextlib import ExitStack

import concourse.mybir as mybir
from concourse.masks import make_identity

K, R, H, T, S, T2, S2, T3, NJ = 1024, 512, 512, 4096, 1024, 2048, 1024, 2048, 512
FLOPS = 2 * (K * R * S + R * H * S + K * H * S + 2 * H * S2 * NJ)

F32 = mybir.dt.float32
BF16 = mybir.dt.bfloat16
I32 = mybir.dt.int32
U32 = mybir.dt.uint32
U16 = mybir.dt.uint16
U8 = mybir.dt.uint8
FP8X4 = mybir.dt.float8_e4m3fn_x4
FP4X4 = mybir.dt.float4_e2m1fn_x4
ACT = mybir.ActivationFunctionType
ALU = mybir.AluOpType

P = 128
PACK = 4
PASS = P * PACK
QUAD = 32
QN = 256
NQ = S // QN
CH = 128
QUADS = (0, 2, 1, 3)


def tile_list_mailbox_suggestion_scores_kernel(
    tc, tab_words, tab_scales, tab2_words, tab2_scales, w1, tgain, w2, w3_words, w3_scales, gain,
    page0, wgs, mat, qry_words, qry_scales, cand, offs, offs2, offs3, offs4, out,
):
    nc = tc.nc
    with ExitStack() as ctx:
        lists = ctx.enter_context(tc.tile_pool(name="lists", bufs=1))
        keep = ctx.enter_context(tc.tile_pool(name="keep", bufs=1))
        ring = ctx.enter_context(tc.tile_pool(name="ring", bufs=2))
        psum = ctx.enter_context(tc.psum_pool(name="psum", bufs=1))

        def held(name, shape, dtype, tag=None):
            return keep.tile(shape, dtype, name=name, tag=tag or name, align_bytes=64)

        def ringed(name, shape, dtype, bufs=2):
            return ring.tile(shape, dtype, name=name, tag=name, bufs=bufs, align_bytes=64)

        def bank(tag, shape, bufs):
            return psum.tile(shape, F32, name=tag, tag=tag, bufs=bufs)

        def words_of(dram):
            return dram.rearrange("p n i -> p (n i)").bitcast(I32)

        idx = lists.tile([P, S // 16], U16, name="idx")
        idx2 = lists.tile([P, S2 // 16], U16, name="idx2")
        idx3 = lists.tile([P, S // 16], U16, name="idx3")
        idx4 = lists.tile([P, NJ // 16], U16, name="idx4")

        tab_w = [held("tab_w%d" % a, [P, T], U32) for a in range(2)]
        tab_s = held("tab_s", [P, T], U8)
        tab2_w = held("tab2_w", [P, T3], U32)
        tab2_s = held("tab2_s", [P, T3], U8)
        w3_raw = held("w3_raw", [P, 2, 2 * H], U8)
        w3s_raw = held("w3s_raw", [P, 2, H], U8)
        v_s1 = held("v_s1", [P, S], U8)
        ident = held("ident", [P, P], F32)
        wgs_raw = held("wgs_raw", [P, S], F32)
        tg = held("tg", [P, PACK], F32)
        gn = held("gn", [P, PACK], F32)
        w1_raw = [held("w1_raw%d" % a, [P, PACK, R], F32) for a in range(2)]

        nc.gpsimd.memset(tab2_s[:].bitcast(I32), 0)
        for plane in (tab_s, w3s_raw, v_s1):
            nc.vector.memset(plane[:].bitcast(I32), 0)
        make_identity(nc, ident[:])
        nc.gpsimd.dma_start(out=gn[:], in_=gain.rearrange("(p t) -> p t", t=PACK))
        for quad in QUADS:
            nc.gpsimd.dma_start(
                out=w3s_raw[QUAD * quad : QUAD * quad + 4, :, :].bitcast(I32),
                in_=w3_scales[:, 4 * quad : 4 * quad + 4, :].rearrange("a r c -> r a c").bitcast(I32),
            )
        nc.gpsimd.dma_start(out=tg[:], in_=tgain.rearrange("(p t) -> p t", t=PACK))

        nc.sync.dma_start(out=tab2_w[:].bitcast(I32), in_=words_of(tab2_words[0]))
        nc.sync.dma_start(idx2[:], offs2)
        for quad in QUADS:
            nc.sync.dma_start(
                out=tab2_s[QUAD * quad + 8 : QUAD * quad + 12, :].bitcast(I32),
                in_=tab2_scales[0, 4 * quad : 4 * quad + 4, :].bitcast(I32),
            )
        nc.sync.dma_start(out=wgs_raw[:], in_=wgs)
        nc.sync.dma_start(out=tab_w[0][:].bitcast(I32), in_=words_of(tab_words[0]))
        nc.sync.dma_start(idx[:], offs)
        for quad in QUADS:
            nc.sync.dma_start(
                out=tab_s[QUAD * quad : QUAD * quad + 8, :].bitcast(I32),
                in_=tab_scales[:, 4 * quad : 4 * quad + 4, :].bitcast(I32),
            )
        w1_rows = w1.rearrange("(a p j) c -> a p j c", a=2, j=PACK)
        nc.sync.dma_start(out=w1_raw[0][:], in_=w1_rows[0])
        nc.sync.dma_start(out=w1_raw[1][:], in_=w1_rows[1])
        nc.sync.dma_start(out=w3_raw[:].bitcast(I32), in_=w3_words.rearrange("a p b -> p a b").bitcast(I32))
        nc.sync.dma_start(idx3[:], offs3)
        nc.sync.dma_start(out=tab_w[1][:].bitcast(I32), in_=words_of(tab_words[1]))
        nc.sync.dma_start(idx4[:], offs4)

        v2_w = held("v2_w", [P, S2], U32)
        v2_s = held("v2_s", [P, S2], U8)
        v_w0 = held("v_w0", [P, S], U32)
        v_s = held("v_s", [P, S], U8)
        nc.vector.tensor_copy(v2_w[:], tab2_w[:].indirect(idx2[:]))
        nc.vector.tensor_copy(v2_s[:], tab2_s[:].indirect(idx2[:]))
        nc.vector.tensor_copy(v_w0[:], tab_w[0][:].indirect(idx[:]))
        w2_raw = held("w2_raw", [P, PACK, H], F32, tag="tab_w0")
        nc.sync.dma_start(out=w2_raw[:], in_=w2.rearrange("(p j) c -> p j c", j=PACK))
        nc.vector.tensor_copy(v_s[:], tab_s[:].indirect(idx[:]))
        for quad in QUADS:
            nc.sync.dma_start(
                out=v_s1[QUAD * quad : QUAD * quad + 4, :].bitcast(I32),
                in_=v_s[QUAD * quad + 4 : QUAD * quad + 8, :].bitcast(I32),
            )

        page_rows = page0.rearrange("(p t) s -> p t s", t=PACK)
        page = []

        def load_page(tag):
            t = len(page)
            rows = held("page%d" % t, [P, T2], F32, tag=tag)
            nc.sync.dma_start(out=rows[:], in_=page_rows[:, t, :])
            page.append(rows)

        load_page("tab_s")

        wg = []
        spread = []
        for half in range(2):
            turned = bank("misc", [P, 4, CH], 4)
            for c in range(4):
                col = (4 * half + c) * CH
                nc.tensor.transpose(turned[:, c, :], wgs_raw[:, col : col + CH], ident[:])
            for c in range(4):
                rep = held("rep%d" % (4 * half + c), [P, PACK, 4, QUAD], F32)
                nc.scalar.copy(
                    out=rep[:],
                    in_=turned[:, c, :].rearrange("j (m t) -> j t m", t=PACK).unsqueeze(2).to_broadcast([P, PACK, 4, QUAD]),
                )
                spread.append(rep)

        def deal_wgs(half, tag):
            wg.append(held("wg%d" % half, [P, PACK, S // 2], F32, tag=tag))
            for t in range(PACK):
                back = bank("misc", [P, 4, CH], 4)
                for c in range(4):
                    nc.tensor.transpose(back[:, c, :], spread[4 * half + c][:, t, :, :].rearrange("j q m -> j (q m)"), ident[:])
                nc.scalar.activation(
                    out=wg[half][:, t, :], in_=back[:].rearrange("p c j -> p (c j)"),
                    func=ACT.Copy, scale=gn[:, t : t + 1],
                )

        deal_wgs(0, "wg0")

        def deal(engine_copy, raw, name, t0, t1, tag=None):
            dealt = held(name, [P, (t1 - t0) * R], BF16, tag=tag)
            engine_copy(
                out=dealt[:].rearrange("p (t m j) -> p m t j", m=P, j=PACK),
                in_=raw[:].rearrange("p j (m t) -> p m t j", t=PACK)[:, :, t0:t1, :],
            )
            return dealt

        def quantize(src, codes, scales):
            nc.vector.quantize_mx(out=codes.bitcast(FP8X4), scales=scales, in_=src)

        w1_c = [held("w1_c0", [P, R], U32)]
        w1_s = [held("w1_s%d" % a, [P, R], U8) for a in range(2)]
        w2_c = [held("w2_c%d" % pair, [P, 2 * P], U32) for pair in range(2)]
        w2_s = [held("w2_s%d" % pair, [P, 2 * P], U8) for pair in range(2)]
        w1_b0 = deal(nc.scalar.copy, w1_raw[0], "w1_b0", 0, PACK)
        deal_wgs(1, "w1_raw0")
        w1_b1 = deal(nc.vector.tensor_copy, w1_raw[1], "w1_b1", 0, PACK)
        load_page("w1_raw1")
        w3_d = held("w3_d", [P, 2, 2 * H], U8)
        nc.vector.tensor_copy(
            out=w3_d[:].bitcast(U16).rearrange("p a (t m) -> p a t m", t=PACK),
            in_=w3_raw[:].bitcast(U16).rearrange("p a (m t) -> p a t m", t=PACK),
        )
        load_page("w3_raw")
        quantize(w1_b0[:], w1_c[0][:], w1_s[0][:])
        w1_c.append(held("w1_c1", [P, R], U32, tag="w1_b0"))
        quantize(w1_b1[:], w1_c[1][:], w1_s[1][:])
        w3s_d = held("w3s_d", [P, 2, H], U8, tag="w1_b1")
        nc.vector.tensor_copy(
            out=w3s_d[:].rearrange("p a (t m) -> p a t m", t=PACK),
            in_=w3s_raw[:].rearrange("p a (m t) -> p a t m", t=PACK),
        )
        v_w1 = held("v_w1", [P, S], U32, tag="w3s_raw")
        for half in range(2):
            nc.vector.tensor_copy(
                v_w1[:, half * S // 2 : (half + 1) * S // 2],
                tab_w[1][:].indirect(idx[:, half * S // 32 : (half + 1) * S // 32]),
            )
        load_page("tab_w1")
        v_w = (v_w0, v_w1)

        def stage1(slices, col, n, tag="acc1", bufs=2):
            acc = bank(tag, [P, len(slices), n], bufs)
            for a in range(2):
                for u, t in enumerate(slices):
                    nc.tensor.matmul_mx(
                        out=acc[:, u, :],
                        lhsT=w1_c[a][:, t * P : (t + 1) * P].bitcast(FP8X4),
                        lhsT_scale=w1_s[a][:, t * P : (t + 1) * P],
                        rhs=v_w[a][:, col : col + n].bitcast(FP8X4),
                        rhs_scale=v_s[4 * a : P, col : col + n],
                        start=(a == 0 and u == 0),
                        stop=(a == 1 and u == len(slices) - 1),
                    )
            return acc

        def act_by_vector():
            th = held("th_first", [P, QN, PACK], F32)
            ab = held("ab_first", [P, QN, PACK], BF16, tag="w2_b0")
            codes, scales = held("act_c_first", [P, QN], U32), held("act_s_first", [P, QN], U8)
            chunks = [slice(c * CH, (c + 1) * CH) for c in range(QN // CH)]
            for cols in chunks:
                acc = stage1(range(PACK), cols.start, CH)
                nc.scalar.activation(out=th[:, cols, :], in_=acc[:].rearrange("p t n -> p n t"), func=ACT.Tanh)
                nc.vector.tensor_tensor(
                    out=ab[:, cols, :], in0=th[:, cols, :],
                    in1=tg[:].unsqueeze(1).to_broadcast([P, CH, PACK]), op=ALU.mult,
                )
            for cols in chunks:
                quantize(ab[:, cols, :].rearrange("p n t -> p (n t)"), codes[:, cols], scales[:, cols])
            return codes, scales, chunks

        def act_by_scalar(q):
            th = ringed("th", [P, PACK, QN], F32, bufs=1)
            sc = held("sc", [P, PACK, QN], BF16, tag="turn%d" % ((q + 1) % 2))
            ab = ringed("ab", [P, QN, PACK], BF16)
            codes, scales = ringed("act_c", [P, QN], U32), ringed("act_s", [P, QN], U8)
            for pair in range(2):
                acc = stage1((0, 1), q * QN, QN) if pair == 0 else stage1((2, 3), q * QN, QN, *(("acc2_0", 1) if q == 1 else ("acc1", 2)))
                nc.scalar.activation(out=th[:, 2 * pair : 2 * pair + 2, :], in_=acc[:], func=ACT.Tanh)
            for t in range(PACK):
                nc.scalar.activation(out=sc[:, t, :], in_=th[:, t, :], func=ACT.Copy, scale=tg[:, t : t + 1])
            nc.scalar.copy(
                out=ab[:].rearrange("p (c i) t -> p c t i", i=4),
                in_=sc[:].rearrange("p t (c i) -> p c t i", i=4),
            )
            quantize(ab[:].rearrange("p n t -> p (n t)"), codes[:], scales[:])
            return codes, scales, [slice(0, QN)]

        def stage2(q, pair, act):
            codes, scales, chunks = act
            acc = bank("acc2_%d" % pair, [P, 2, QN], 1)
            cols = slice(q * QN, (q + 1) * QN)
            for a in range(2):
                for u in range(2):
                    t = 2 * pair + u
                    nc.tensor.matmul_mx(
                        out=acc[:, u, :],
                        lhsT=w3_d[:, a, 2 * t * P : 2 * (t + 1) * P].bitcast(FP4X4),
                        lhsT_scale=w3s_d[:, a, t * P : (t + 1) * P],
                        rhs=v_w[a][:, cols].bitcast(FP8X4),
                        rhs_scale=(v_s, v_s1)[a][:, cols],
                        start=(u == 0 and a == 0),
                        stop=False,
                    )
            for part in chunks:
                for u in range(2):
                    nc.tensor.matmul_mx(
                        out=acc[:, u, part],
                        lhsT=w2_c[pair][:, u * P : (u + 1) * P].bitcast(FP8X4),
                        lhsT_scale=w2_s[pair][:, u * P : (u + 1) * P],
                        rhs=codes[:, part].bitcast(FP8X4),
                        rhs_scale=scales[:, part],
                        start=False,
                        stop=(u == 1 and part.stop == QN),
                    )
            return acc

        def put(q, pair, acc):
            hs = held("hs", [P, 2, QN], F32, tag=("hs%d", "turn%d")[pair] % (q % 2))
            for part in (slice(0, 1), slice(1, 2)) if q == 0 and pair == 0 else (slice(0, 2),):
                nc.scalar.copy(out=hs[:, part, :], in_=acc[:, part, :])
            for u in range(2):
                t = 2 * pair + u
                nc.vector.tensor_tensor(
                    page[t][:].indirect(idx3[:, q * QN // 16 : (q + 1) * QN // 16]),
                    hs[:, u, :], wg[q // 2][:, t, (q % 2) * QN : (q % 2 + 1) * QN], ALU.mult,
                )

        w2_b0 = deal(nc.vector.tensor_copy, w2_raw, "w2_b0", 0, 2)
        quantize(w2_b0[:], w2_c[0][:], w2_s[0][:])
        act = act_by_vector()
        first = stage2(0, 0, act)
        w2_b1 = deal(nc.vector.tensor_copy, w2_raw, "w2_b1", 2, PACK, "th_first")
        quantize(w2_b1[:], w2_c[1][:], w2_s[1][:])
        second = stage2(0, 1, act)

        mat_sb = held("mat_sb", [P, PACK, NJ], F32, tag="tab_w0")
        nc.sync.dma_start(out=mat_sb[:], in_=mat.rearrange("(p t) j -> p t j", t=PACK))
        qry_w = held("qry_w", [P, NJ], U32, tag="w2_b0")
        nc.sync.dma_start(out=qry_w[:].bitcast(I32), in_=words_of(qry_words[0]))
        qry_s = held("qry_s", [P, NJ], U8, tag="th_first")
        nc.gpsimd.memset(qry_s[:].bitcast(I32), 0)
        for quad in QUADS:
            nc.sync.dma_start(
                out=qry_s[QUAD * quad : QUAD * quad + 4, :].bitcast(I32),
                in_=qry_scales[0, 4 * quad : 4 * quad + 4, :].bitcast(I32),
            )

        cand_rows = held("cand_rows", [P, P], F32, tag="act_c_first")
        nc.gpsimd.memset(cand_rows[:], 0.0)
        nc.sync.dma_start(out=cand_rows[0 : S2 // P, :], in_=cand.rearrange("(i p) -> i p", p=P))

        for q in range(NQ):
            put(q, 0, first)
            if q + 1 < NQ:
                act = act_by_scalar(q + 1)
                first = stage2(q + 1, 0, act)
            put(q, 1, second)
            if q + 1 < NQ:
                second = stage2(q + 1, 1, act)

        cand_t = bank("acc1", [P, P], 2)
        nc.tensor.transpose(cand_t[:], cand_rows[:], ident[:])
        cd = held("cd", [P, S2 // P], F32)
        nc.scalar.copy(out=cd[:], in_=cand_t[:, 0 : S2 // P])

        def against_candidates(i, codes, scales, tag, bufs, parts):
            acc = bank(tag, [P, NJ], bufs)
            for part in parts:
                nc.tensor.matmul_mx(
                    out=acc[:, part],
                    lhsT=v2_w[:, i * P : (i + 1) * P].bitcast(FP8X4),
                    lhsT_scale=v2_s[8:P, i * P : (i + 1) * P],
                    rhs=codes[:, part].bitcast(FP8X4),
                    rhs_scale=scales[:, part],
                    start=True,
                    stop=True,
                )
            return acc

        whole = [slice(0, NJ)]
        halves = [slice(0, NJ // 2), slice(NJ // 2, NJ)]
        best = []
        for i in range(S2 // P):
            acc = against_candidates(i, qry_w, qry_s, "acc1", 2, whole)
            row = held("best%d" % i, [P, NJ], F32)
            nc.scalar.activation(out=row[:], in_=acc[:], func=ACT.Identity, bias=cd[:, i : i + 1])
            best.append(row)

        x_f = held("x_f", [P, PACK, NJ], F32)
        for t in range(PACK):
            for part in halves if t == PACK - 1 else whole:
                nc.vector.tensor_tensor(
                    x_f[:, t, part], page[t][:].indirect(idx4[:, part.start // 16 : part.stop // 16]),
                    mat_sb[:, t, part], ALU.mult,
                )
        x_b = held("x_b", [P, NJ, PACK], BF16)
        x_c = held("x_c", [P, NJ], U32, tag="w2_b0")
        x_s = held("x_s", [P, NJ], U8)
        for part in halves:
            nc.vector.tensor_copy(
                out=x_b[:, part, :].rearrange("p (c i) t -> p c t i", i=4),
                in_=x_f[:, :, part].rearrange("p t (c i) -> p c t i", i=4),
            )
        for part in halves:
            quantize(x_b[:, part, :].rearrange("p n t -> p (n t)"), x_c[:, part], x_s[:, part])
        for i in range(S2 // P):
            for part in halves if i in (0, S2 // P - 1) else whole:
                acc = against_candidates(i, x_c, x_s, "misc", 4, [part])
                nc.vector.scalar_tensor_tensor(
                    out=best[i][:, part], in0=acc[:, part], scalar=cd[:, i : i + 1], in1=best[i][:, part],
                    op0=ALU.add, op1=ALU.max,
                )
                nc.sync.dma_start(out=out[i * P : (i + 1) * P, part], in_=best[i][:, part])
